import numpy as np, ml_dtypes
CORES = [0,1,2,3,4,5,6,7,128,129,130,131,132,133,134,135]
N = 16
TK = 512
def setup_inputs(rng):
    return {"x": rng.standard_normal((N, 128, TK), dtype=np.float32).astype(ml_dtypes.bfloat16), "w1": rng.standard_normal((N, 128, 128), dtype=np.float32).astype(ml_dtypes.bfloat16), "w2": rng.standard_normal((N, 128, 128), dtype=np.float32).astype(ml_dtypes.bfloat16)}
def reference(x, w1, w2):
    tot = np.zeros((128, TK))
    for r in range(N):
        h = np.maximum(w1[r].astype(np.float64).T @ x[r].astype(np.float64), 0.0)
        tot += w2[r].astype(np.float64).T @ h
    s = tot.astype(ml_dtypes.bfloat16 if x.dtype != np.float64 else np.float64)
    return {"y": np.broadcast_to(s, (N,) + s.shape)}

@@ -1,0 +1,104 @@
+from concourse.bass import DstId, RemoteDMATransfer
+from concourse.mybir import AluOpType
+
+W = 64
+B = 128
+OWNER = [0, 1, 4, 5, 2, 3, 6, 7]
+
+SCRATCH = {
+    "xs": ("sbuf", [128, 512], "bfloat16"),
+    "w1s": ("sbuf", [128, 128], "bfloat16"),
+    "w2s": ("sbuf", [128, 128], "bfloat16"),
+    "zero": ("sbuf", [128, B], "float32"),
+    "h": ("sbuf", [128, 512], "bfloat16"),
+    "pbf": ("sbuf", [128, 512], "bfloat16"),
+    "land": ("sbuf", [128, 512], "bfloat16"),
+    "peer": ("sbuf", [128, W], "bfloat16"),
+    "t": ("sbuf", [128, 448], "float32"),
+    "ybuf": ("sbuf", [128, 512], "bfloat16"),
+    "z0": ("psum", [128, 512], "float32"), "z1": ("psum", [128, 512], "float32"),
+    "z2": ("psum", [128, 512], "float32"), "z3": ("psum", [128, 512], "float32"),
+    "p0": ("psum", [128, 512], "float32"), "p1": ("psum", [128, 512], "float32"),
+    "p2": ("psum", [128, 512], "float32"), "p3": ("psum", [128, 512], "float32"),
+}
+SEMAPHORES = ["ld", "vz", "zs", "hs", "ps", "pc", "rs", "px", "tv", "fin", "ag", "sent", "st"]
+
+
+def rank_program(g, core, T, topo):
+    if T.rank_of(core) is None:
+        return
+    S = T.sem
+    me = core % 8
+    base = core - me
+    mine = OWNER.index(me)
+    my_cols = slice(W * mine, W * mine + W)
+    zp = [T.z0, T.z1, T.z2, T.z3]
+    pp = [T.p0, T.p1, T.p2, T.p3]
+
+    def dst_id(d):
+        rid, pid = topo.addr(d, core)
+        return DstId(rid=rid, pnc=pid)
+
+    g.sync.dma_start(T.w1s[:], T.w1[:]).then_inc(S.ld, 16)
+    g.sync.dma_start(T.xs[:], T.x[:]).then_inc(S.ld, 16)
+    g.sync.dma_start(T.w2s[:], T.w2[:]).then_inc(S.ld, 16)
+
+    te = g.tensor
+    te.wait_ge(S.ld, 48)
+    for half in (0, 1):
+        for q in (2 * half, 2 * half + 1):
+            te.matmul(zp[q][:, 0:B], T.w1s[:], T.xs[:, B * q:B * q + B], True, True).then_inc(S.zs, 1)
+        for q in (2 * half, 2 * half + 1):
+            te.wait_ge(S.hs, q + 1)
+            te.matmul(pp[q][:, 0:B], T.w2s[:], T.h[:, B * q:B * q + B], True, True).then_inc(S.ps, 1)
+
+    ve = g.vector
+    ve.memset(T.zero[:], 0.0).then_inc(S.vz, 1)
+    ve.wait_ge(S.vz, 1)
+    for half in (0, 1):
+        for q in (2 * half, 2 * half + 1):
+            ve.wait_ge(S.zs, q + 1)
+            ve.tensor_tensor(T.h[:, B * q:B * q + B], zp[q][:, 0:B], T.zero[:], AluOpType.max).then_inc(S.hs, 1)
+        for q in (2 * half, 2 * half + 1):
+            ve.wait_ge(S.ps, q + 1)
+            ve.tensor_copy(T.pbf[:, B * q:B * q + B], pp[q][:, 0:B]).then_inc(S.pc, 1)
+    ve.wait_ge(S.pc, 4)
+    ve.tensor_copy(T.land[:, W * me:W * me + W], T.pbf[:, my_cols]).then_inc(S.tv, 1)
+    ve.wait_ge(S.tv, 1)
+    ve.wait_ge(S.rs, 28)
+    ve.tensor_tensor(T.t[:, 0:256], T.land[:, 0:256], T.land[:, 256:512], AluOpType.add).then_inc(S.tv, 1)
+    ve.wait_ge(S.tv, 2)
+    ve.tensor_tensor(T.t[:, 256:384], T.t[:, 0:128], T.t[:, 128:256], AluOpType.add).then_inc(S.tv, 1)
+    ve.wait_ge(S.tv, 3)
+    ve.tensor_tensor(T.t[:, 384:448], T.t[:, 256:320], T.t[:, 320:384], AluOpType.add).then_inc(S.tv, 1)
+    ve.wait_ge(S.tv, 4)
+    ve.wait_ge(S.px, 8)
+    ve.tensor_tensor(T.ybuf[:, my_cols], T.t[:, 384:448], T.peer[:], AluOpType.add).then_inc(S.fin, 1)
+
+    for half in (0, 1):
+        g.wait_ge(S.pc, 2 * half + 2)
+        tr = []
+        for k in range(4):
+            s = 4 * half + k
+            if s == mine:
+                continue
+            tr.append(RemoteDMATransfer(dst_ids=[dst_id(base + OWNER[s])], dma_engine_mask=0xF << (4 * k),
+                                        remote_sem=S.rs, src=T.pbf[:, W * s:W * s + W],
+                                        dst=T.land[:, W * me:W * me + W]))
+        g.remote_dma_fused(tr, local_sem=S.sent)
+        if mine // 4 == half:
+            other = core ^ 128
+            g.wait_ge(S.rs, 28)
+            srcs = [T.pbf[:, my_cols]] + [T.land[:, W * i:W * i + W] for i in range(8) if i != me]
+            g.remote_dma_fused([RemoteDMATransfer(dst_ids=[dst_id(other)], dma_engine_mask=topo.mask(core, other),
+                                                  remote_sem=S.px, srcs=srcs, dsts=[T.peer[:]], alu_op=1)],
+                               local_sem=S.sent)
+    others = [base + i for i in range(8) if i != me]
+    g.wait_ge(S.fin, 1)
+    g.remote_dma_fused([RemoteDMATransfer(dst_ids=[dst_id(d) for d in others], dma_engine_mask=0xFFFF, remote_sem=S.ag,
+                                          srcs=[T.ybuf[:, my_cols]], dsts=[T.ybuf[:, my_cols] for d in others])],
+                       local_sem=S.sent)
+    g.wait_ge(S.ag, 7 * 16)
+    g.dma_start(T.y[:], T.ybuf[:]).then_inc(S.st, 16)
+    g.wait_ge(S.st, 16)
+    g.wait_ge(S.sent, 7 * 4 + 8 + 16)

@@ -2,24 +2,22 @@ from concourse.bass import DstId, RemoteDMATransfer
 from concourse.mybir import AluOpType
 
 W = 64
-B = 128
-OWNER = [0, 1, 4, 5, 2, 3, 6, 7]
+EARLY = 3
+OWNER = [0, 4, 1, 5, 2, 6, 3, 7]
 
 SCRATCH = {
     "xs": ("sbuf", [128, 512], "bfloat16"),
     "w1s": ("sbuf", [128, 128], "bfloat16"),
     "w2s": ("sbuf", [128, 128], "bfloat16"),
-    "zero": ("sbuf", [128, B], "float32"),
+    "zero": ("sbuf", [128, 256], "float32"),
     "h": ("sbuf", [128, 512], "bfloat16"),
     "pbf": ("sbuf", [128, 512], "bfloat16"),
     "land": ("sbuf", [128, 512], "bfloat16"),
     "peer": ("sbuf", [128, W], "bfloat16"),
     "t": ("sbuf", [128, 448], "float32"),
     "ybuf": ("sbuf", [128, 512], "bfloat16"),
-    "z0": ("psum", [128, 512], "float32"), "z1": ("psum", [128, 512], "float32"),
-    "z2": ("psum", [128, 512], "float32"), "z3": ("psum", [128, 512], "float32"),
-    "p0": ("psum", [128, 512], "float32"), "p1": ("psum", [128, 512], "float32"),
-    "p2": ("psum", [128, 512], "float32"), "p3": ("psum", [128, 512], "float32"),
+    "z0": ("psum", [128, 512], "float32"), "z1": ("psum", [128, 512], "float32"), "z2": ("psum", [128, 512], "float32"),
+    "p0": ("psum", [128, 512], "float32"), "p1": ("psum", [128, 512], "float32"), "p2": ("psum", [128, 512], "float32"),
 }
 SEMAPHORES = ["ld", "vz", "zs", "hs", "ps", "pc", "rs", "px", "tv", "fin", "ag", "sent", "st"]
 
@@ -31,9 +29,16 @@ def rank_program(g, core, T, topo):
     me = core % 8
     base = core - me
     mine = OWNER.index(me)
+    early = mine < EARLY
     my_cols = slice(W * mine, W * mine + W)
-    zp = [T.z0, T.z1, T.z2, T.z3]
-    pp = [T.p0, T.p1, T.p2, T.p3]
+    zp = [T.z0, T.z1, T.z2]
+    pp = [T.p0, T.p1, T.p2]
+
+    if early:
+        stages = [([(0, 256), (256, 512)], list(range(8)))]
+    else:
+        stages = [([(0, 64), (64, 128), (128, 192)], list(range(EARLY))),
+                  ([(192, 320), (320, 448), (448, 512)], list(range(EARLY, 8)))]
 
     def dst_id(d):
         rid, pid = topo.addr(d, core)
@@ -45,27 +50,35 @@ def rank_program(g, core, T, topo):
 
     te = g.tensor
     te.wait_ge(S.ld, 48)
-    for half in (0, 1):
-        for q in (2 * half, 2 * half + 1):
-            te.matmul(zp[q][:, 0:B], T.w1s[:], T.xs[:, B * q:B * q + B], True, True).then_inc(S.zs, 1)
-        for q in (2 * half, 2 * half + 1):
-            te.wait_ge(S.hs, q + 1)
-            te.matmul(pp[q][:, 0:B], T.w2s[:], T.h[:, B * q:B * q + B], True, True).then_inc(S.ps, 1)
+    n = 0
+    for blocks, slices in stages:
+        if n:
+            te.wait_ge(S.pc, n)
+        for k, (a, b) in enumerate(blocks):
+            te.matmul(zp[k][:, 0:b - a], T.w1s[:], T.xs[:, a:b], True, True).then_inc(S.zs, 1)
+        for k, (a, b) in enumerate(blocks):
+            te.wait_ge(S.hs, n + k + 1)
+            te.matmul(pp[k][:, 0:b - a], T.w2s[:], T.h[:, a:b], True, True).then_inc(S.ps, 1)
+        n += len(blocks)
+    nblocks = n
 
     ve = g.vector
     ve.memset(T.zero[:], 0.0).then_inc(S.vz, 1)
     ve.wait_ge(S.vz, 1)
-    for half in (0, 1):
-        for q in (2 * half, 2 * half + 1):
-            ve.wait_ge(S.zs, q + 1)
-            ve.tensor_tensor(T.h[:, B * q:B * q + B], zp[q][:, 0:B], T.zero[:], AluOpType.max).then_inc(S.hs, 1)
-        for q in (2 * half, 2 * half + 1):
-            ve.wait_ge(S.ps, q + 1)
-            ve.tensor_copy(T.pbf[:, B * q:B * q + B], pp[q][:, 0:B]).then_inc(S.pc, 1)
-    ve.wait_ge(S.pc, 4)
+    n = 0
+    for blocks, slices in stages:
+        for k, (a, b) in enumerate(blocks):
+            ve.wait_ge(S.zs, n + k + 1)
+            ve.tensor_tensor(T.h[:, a:b], zp[k][:, 0:b - a], T.zero[:, 0:b - a], AluOpType.max).then_inc(S.hs, 1)
+        for k, (a, b) in enumerate(blocks):
+            ve.wait_ge(S.ps, n + k + 1)
+            ve.tensor_copy(T.pbf[:, a:b], pp[k][:, 0:b - a]).then_inc(S.pc, 1)
+        n += len(blocks)
+    rs_all = 2 * (EARLY - 1) + 4 * (8 - EARLY) if early else 2 * EARLY + 4 * (8 - EARLY - 1)
+    ve.wait_ge(S.pc, nblocks)
     ve.tensor_copy(T.land[:, W * me:W * me + W], T.pbf[:, my_cols]).then_inc(S.tv, 1)
     ve.wait_ge(S.tv, 1)
-    ve.wait_ge(S.rs, 28)
+    ve.wait_ge(S.rs, rs_all)
     ve.tensor_tensor(T.t[:, 0:256], T.land[:, 0:256], T.land[:, 256:512], AluOpType.add).then_inc(S.tv, 1)
     ve.wait_ge(S.tv, 2)
     ve.tensor_tensor(T.t[:, 256:384], T.t[:, 0:128], T.t[:, 128:256], AluOpType.add).then_inc(S.tv, 1)
@@ -75,24 +88,28 @@ def rank_program(g, core, T, topo):
     ve.wait_ge(S.px, 8)
     ve.tensor_tensor(T.ybuf[:, my_cols], T.t[:, 384:448], T.peer[:], AluOpType.add).then_inc(S.fin, 1)
 
-    for half in (0, 1):
-        g.wait_ge(S.pc, 2 * half + 2)
+    eng = 2 if early else 4
+    n = 0
+    sent = 0
+    for blocks, slices in stages:
+        n += len(blocks)
+        g.wait_ge(S.pc, n)
         tr = []
-        for k in range(4):
-            s = 4 * half + k
+        for s in slices:
             if s == mine:
                 continue
-            tr.append(RemoteDMATransfer(dst_ids=[dst_id(base + OWNER[s])], dma_engine_mask=0xF << (4 * k),
+            tr.append(RemoteDMATransfer(dst_ids=[dst_id(base + OWNER[s])],
+                                        dma_engine_mask=((1 << eng) - 1) << (eng * len(tr)),
                                         remote_sem=S.rs, src=T.pbf[:, W * s:W * s + W],
                                         dst=T.land[:, W * me:W * me + W]))
         g.remote_dma_fused(tr, local_sem=S.sent)
-        if mine // 4 == half:
-            other = core ^ 128
-            g.wait_ge(S.rs, 28)
-            srcs = [T.pbf[:, my_cols]] + [T.land[:, W * i:W * i + W] for i in range(8) if i != me]
-            g.remote_dma_fused([RemoteDMATransfer(dst_ids=[dst_id(other)], dma_engine_mask=topo.mask(core, other),
-                                                  remote_sem=S.px, srcs=srcs, dsts=[T.peer[:]], alu_op=1)],
-                               local_sem=S.sent)
+        sent += eng * len(tr)
+    other = core ^ 128
+    g.wait_ge(S.rs, rs_all)
+    srcs = [T.pbf[:, my_cols]] + [T.land[:, W * i:W * i + W] for i in range(8) if i != me]
+    g.remote_dma_fused([RemoteDMATransfer(dst_ids=[dst_id(other)], dma_engine_mask=topo.mask(core, other),
+                                          remote_sem=S.px, srcs=srcs, dsts=[T.peer[:]], alu_op=1)],
+                       local_sem=S.sent)
     others = [base + i for i in range(8) if i != me]
     g.wait_ge(S.fin, 1)
     g.remote_dma_fused([RemoteDMATransfer(dst_ids=[dst_id(d) for d in others], dma_engine_mask=0xFFFF, remote_sem=S.ag,
@@ -101,4 +118,4 @@ def rank_program(g, core, T, topo):
     g.wait_ge(S.ag, 7 * 16)
     g.dma_start(T.y[:], T.ybuf[:]).then_inc(S.st, 16)
     g.wait_ge(S.st, 16)
-    g.wait_ge(S.sent, 7 * 4 + 8 + 16)
+    g.wait_ge(S.sent, sent + 8 + 16)

@@ -4,6 +4,7 @@ from concourse.mybir import AluOpType
 W = 64
 EARLY = 3
 OWNER = [0, 4, 1, 5, 2, 6, 3, 7]
+NZ, NP = 3, 5
 
 SCRATCH = {
     "xs": ("sbuf", [128, 512], "bfloat16"),
@@ -18,8 +19,13 @@ SCRATCH = {
     "ybuf": ("sbuf", [128, 512], "bfloat16"),
     "z0": ("psum", [128, 512], "float32"), "z1": ("psum", [128, 512], "float32"), "z2": ("psum", [128, 512], "float32"),
     "p0": ("psum", [128, 512], "float32"), "p1": ("psum", [128, 512], "float32"), "p2": ("psum", [128, 512], "float32"),
+    "p3": ("psum", [128, 512], "float32"), "p4": ("psum", [128, 512], "float32"),
 }
 SEMAPHORES = ["ld", "vz", "zs", "hs", "ps", "pc", "rs", "px", "tv", "fin", "ag", "sent", "st"]
+
+
+def cut(a, b, w):
+    return [(c, min(c + w, b)) for c in range(a, b, w)]
 
 
 def rank_program(g, core, T, topo):
@@ -32,13 +38,14 @@ def rank_program(g, core, T, topo):
     early = mine < EARLY
     my_cols = slice(W * mine, W * mine + W)
     zp = [T.z0, T.z1, T.z2]
-    pp = [T.p0, T.p1, T.p2]
+    pp = [T.p0, T.p1, T.p2, T.p3, T.p4]
 
+    E = W * EARLY
     if early:
-        stages = [([(0, 256), (256, 512)], list(range(8)))]
+        stages = [(cut(0, 512, 256), cut(0, 512, 128), list(range(8)))]
     else:
-        stages = [([(0, 64), (64, 128), (128, 192)], list(range(EARLY))),
-                  ([(192, 320), (320, 448), (448, 512)], list(range(EARLY, 8)))]
+        stages = [(cut(0, E, 64), cut(0, E, 64), list(range(EARLY))),
+                  (cut(E, 512, 128), cut(E, 512, 64), list(range(EARLY, 8)))]
 
     def dst_id(d):
         rid, pid = topo.addr(d, core)
@@ -49,33 +56,37 @@ def rank_program(g, core, T, topo):
     g.sync.dma_start(T.w2s[:], T.w2[:]).then_inc(S.ld, 16)
 
     te = g.tensor
-    te.wait_ge(S.ld, 48)
-    n = 0
-    for blocks, slices in stages:
-        if n:
-            te.wait_ge(S.pc, n)
-        for k, (a, b) in enumerate(blocks):
-            te.matmul(zp[k][:, 0:b - a], T.w1s[:], T.xs[:, a:b], True, True).then_inc(S.zs, 1)
-        for k, (a, b) in enumerate(blocks):
-            te.wait_ge(S.hs, n + k + 1)
-            te.matmul(pp[k][:, 0:b - a], T.w2s[:], T.h[:, a:b], True, True).then_inc(S.ps, 1)
-        n += len(blocks)
-    nblocks = n
-
     ve = g.vector
+    te.wait_ge(S.ld, 48)
     ve.memset(T.zero[:], 0.0).then_inc(S.vz, 1)
     ve.wait_ge(S.vz, 1)
-    n = 0
-    for blocks, slices in stages:
-        for k, (a, b) in enumerate(blocks):
-            ve.wait_ge(S.zs, n + k + 1)
-            ve.tensor_tensor(T.h[:, a:b], zp[k][:, 0:b - a], T.zero[:, 0:b - a], AluOpType.max).then_inc(S.hs, 1)
-        for k, (a, b) in enumerate(blocks):
-            ve.wait_ge(S.ps, n + k + 1)
-            ve.tensor_copy(T.pbf[:, a:b], pp[k][:, 0:b - a]).then_inc(S.pc, 1)
-        n += len(blocks)
+    zi = 0
+    pi = 0
+    for zb, pb, slices in stages:
+        if pi:
+            te.wait_ge(S.pc, pi)
+        z_first = zi
+        for a, b in zb:
+            bank = zp[zi % NZ]
+            if zi >= NZ:
+                te.wait_ge(S.hs, zi - NZ + 1)
+            te.matmul(bank[:, 0:b - a], T.w1s[:], T.xs[:, a:b], True, True).then_inc(S.zs, 1)
+            ve.wait_ge(S.zs, zi + 1)
+            ve.tensor_tensor(T.h[:, a:b], bank[:, 0:b - a], T.zero[:, 0:b - a], AluOpType.max).then_inc(S.hs, 1)
+            zi += 1
+        for a, b in pb:
+            bank = pp[pi % NP]
+            te.wait_ge(S.hs, z_first + 1 + min(i for i, zz in enumerate(zb) if zz[1] >= b))
+            if pi >= NP:
+                te.wait_ge(S.pc, pi - NP + 1)
+            te.matmul(bank[:, 0:b - a], T.w2s[:], T.h[:, a:b], True, True).then_inc(S.ps, 1)
+            ve.wait_ge(S.ps, pi + 1)
+            ve.tensor_copy(T.pbf[:, a:b], bank[:, 0:b - a]).then_inc(S.pc, 1)
+            pi += 1
+
     rs_all = 2 * (EARLY - 1) + 4 * (8 - EARLY) if early else 2 * EARLY + 4 * (8 - EARLY - 1)
-    ve.wait_ge(S.pc, nblocks)
+
+    ve.wait_ge(S.pc, pi)
     ve.tensor_copy(T.land[:, W * me:W * me + W], T.pbf[:, my_cols]).then_inc(S.tv, 1)
     ve.wait_ge(S.tv, 1)
     ve.wait_ge(S.rs, rs_all)
@@ -91,8 +102,8 @@ def rank_program(g, core, T, topo):
     eng = 2 if early else 4
     n = 0
     sent = 0
-    for blocks, slices in stages:
-        n += len(blocks)
+    for zb, pb, slices in stages:
+        n += len(pb)
         g.wait_ge(S.pc, n)
         tr = []
         for s in slices:

from concourse.bass import DstId, RemoteDMATransfer
from concourse.mybir import AluOpType

W = 64
EARLY = 3
OWNER = [0, 4, 1, 5, 2, 6, 3, 7]
NZ, NP = 3, 5

SCRATCH = {
    "xs": ("sbuf", [128, 512], "bfloat16"),
    "w1s": ("sbuf", [128, 128], "bfloat16"),
    "w2s": ("sbuf", [128, 128], "bfloat16"),
    "zero": ("sbuf", [128, 256], "float32"),
    "h": ("sbuf", [128, 512], "bfloat16"),
    "pbf": ("sbuf", [128, 512], "bfloat16"),
    "land": ("sbuf", [128, 512], "bfloat16"),
    "peer": ("sbuf", [128, W], "bfloat16"),
    "t": ("sbuf", [128, 448], "float32"),
    "ybuf": ("sbuf", [128, 512], "bfloat16"),
    "z0": ("psum", [128, 512], "float32"), "z1": ("psum", [128, 512], "float32"), "z2": ("psum", [128, 512], "float32"),
    "p0": ("psum", [128, 512], "float32"), "p1": ("psum", [128, 512], "float32"), "p2": ("psum", [128, 512], "float32"),
    "p3": ("psum", [128, 512], "float32"), "p4": ("psum", [128, 512], "float32"),
}
SEMAPHORES = ["ld", "vz", "zs", "hs", "ps", "pc", "rs", "px", "tv", "fin", "ag", "sent", "st"]


def cut(a, b, w):
    return [(c, min(c + w, b)) for c in range(a, b, w)]


def rank_program(g, core, T, topo):
    if T.rank_of(core) is None:
        return
    S = T.sem
    me = core % 8
    base = core - me
    mine = OWNER.index(me)
    early = mine < EARLY
    my_cols = slice(W * mine, W * mine + W)
    zp = [T.z0, T.z1, T.z2]
    pp = [T.p0, T.p1, T.p2, T.p3, T.p4]

    E = W * EARLY
    if early:
        stages = [(cut(0, 512, 256), cut(0, 512, 128), list(range(8)))]
    else:
        stages = [(cut(0, E, 64), cut(0, E, 64), list(range(EARLY))),
                  (cut(E, 512, 128), cut(E, 512, 64), list(range(EARLY, 8)))]

    def dst_id(d):
        rid, pid = topo.addr(d, core)
        return DstId(rid=rid, pnc=pid)

    g.sync.dma_start(T.w1s[:], T.w1[:]).then_inc(S.ld, 16)
    g.sync.dma_start(T.xs[:], T.x[:]).then_inc(S.ld, 16)
    g.sync.dma_start(T.w2s[:], T.w2[:]).then_inc(S.ld, 16)

    te = g.tensor
    ve = g.vector
    te.wait_ge(S.ld, 48)
    ve.memset(T.zero[:], 0.0).then_inc(S.vz, 1)
    ve.wait_ge(S.vz, 1)
    zi = 0
    pi = 0
    for zb, pb, slices in stages:
        if pi:
            te.wait_ge(S.pc, pi)
        z_first = zi
        for a, b in zb:
            bank = zp[zi % NZ]
            if zi >= NZ:
                te.wait_ge(S.hs, zi - NZ + 1)
            te.matmul(bank[:, 0:b - a], T.w1s[:], T.xs[:, a:b], True, True).then_inc(S.zs, 1)
            ve.wait_ge(S.zs, zi + 1)
            ve.tensor_tensor(T.h[:, a:b], bank[:, 0:b - a], T.zero[:, 0:b - a], AluOpType.max).then_inc(S.hs, 1)
            zi += 1
        for a, b in pb:
            bank = pp[pi % NP]
            te.wait_ge(S.hs, z_first + 1 + min(i for i, zz in enumerate(zb) if zz[1] >= b))
            if pi >= NP:
                te.wait_ge(S.pc, pi - NP + 1)
            te.matmul(bank[:, 0:b - a], T.w2s[:], T.h[:, a:b], True, True).then_inc(S.ps, 1)
            ve.wait_ge(S.ps, pi + 1)
            ve.tensor_copy(T.pbf[:, a:b], bank[:, 0:b - a]).then_inc(S.pc, 1)
            pi += 1

    rs_all = 2 * (EARLY - 1) + 4 * (8 - EARLY) if early else 2 * EARLY + 4 * (8 - EARLY - 1)

    ve.wait_ge(S.pc, pi)
    ve.tensor_copy(T.land[:, W * me:W * me + W], T.pbf[:, my_cols]).then_inc(S.tv, 1)
    ve.wait_ge(S.tv, 1)
    ve.wait_ge(S.rs, rs_all)
    ve.tensor_tensor(T.t[:, 0:256], T.land[:, 0:256], T.land[:, 256:512], AluOpType.add).then_inc(S.tv, 1)
    ve.wait_ge(S.tv, 2)
    ve.tensor_tensor(T.t[:, 256:384], T.t[:, 0:128], T.t[:, 128:256], AluOpType.add).then_inc(S.tv, 1)
    ve.wait_ge(S.tv, 3)
    ve.tensor_tensor(T.t[:, 384:448], T.t[:, 256:320], T.t[:, 320:384], AluOpType.add).then_inc(S.tv, 1)
    ve.wait_ge(S.tv, 4)
    ve.wait_ge(S.px, 8)
    ve.tensor_tensor(T.ybuf[:, my_cols], T.t[:, 384:448], T.peer[:], AluOpType.add).then_inc(S.fin, 1)

    eng = 2 if early else 4
    n = 0
    sent = 0
    for zb, pb, slices in stages:
        n += len(pb)
        g.wait_ge(S.pc, n)
        tr = []
        for s in slices:
            if s == mine:
                continue
            tr.append(RemoteDMATransfer(dst_ids=[dst_id(base + OWNER[s])],
                                        dma_engine_mask=((1 << eng) - 1) << (eng * len(tr)),
                                        remote_sem=S.rs, src=T.pbf[:, W * s:W * s + W],
                                        dst=T.land[:, W * me:W * me + W]))
        g.remote_dma_fused(tr, local_sem=S.sent)
        sent += eng * len(tr)
    other = core ^ 128
    g.wait_ge(S.rs, rs_all)
    srcs = [T.pbf[:, my_cols]] + [T.land[:, W * i:W * i + W] for i in range(8) if i != me]
    g.remote_dma_fused([RemoteDMATransfer(dst_ids=[dst_id(other)], dma_engine_mask=topo.mask(core, other),
                                          remote_sem=S.px, srcs=srcs, dsts=[T.peer[:]], alu_op=1)],
                       local_sem=S.sent)
    others = [base + i for i in range(8) if i != me]
    g.wait_ge(S.fin, 1)
    g.remote_dma_fused([RemoteDMATransfer(dst_ids=[dst_id(d) for d in others], dma_engine_mask=0xFFFF, remote_sem=S.ag,
                                          srcs=[T.ybuf[:, my_cols]], dsts=[T.ybuf[:, my_cols] for d in others])],
                       local_sem=S.sent)
    g.wait_ge(S.ag, 7 * 16)
    g.dma_start(T.y[:], T.ybuf[:]).then_inc(S.st, 16)
    g.wait_ge(S.st, 16)
    g.wait_ge(S.sent, sent + 8 + 16)
